import numpy as np
import ml_dtypes


def mxq(x, axis, fmt="e4m3"):
    dtype, down = {"e4m3": (ml_dtypes.float8_e4m3fn, 7), "e5m2": (ml_dtypes.float8_e5m2, 14)}[fmt]
    v = np.moveaxis(np.asarray(x, np.float32).astype(ml_dtypes.bfloat16).astype(np.float64), axis, -1)
    blocks = v.reshape(v.shape[:-1] + (-1, 32))
    amax = np.abs(blocks).max(-1, keepdims=True)
    byte = np.maximum(np.where(amax > 0, np.frexp(amax)[1] - 1 + 127, 0) - down, 1)
    scale = np.exp2(byte - 127.0)
    codes = (blocks / scale).astype(np.float32).astype(dtype).astype(np.float64)
    return np.moveaxis((codes * scale).reshape(v.shape), -1, axis)


WIDE = False


def mx_kscale(k):
    if not WIDE:
        return np.ones(k)
    levels = np.array([10, -10, 5, -5, 0])
    if k % 512:
        return np.exp2(np.random.permutation(np.resize(levels, k // 32))).repeat(32)
    a = np.empty((k // 512, 16))
    for p in range(k // 512):
        a[p, :8] = np.random.permutation(np.resize(levels, 8))
        for g in range(8):
            far = levels[np.abs(levels - a[p, g]) >= 10]
            a[p, g + 8] = far[np.random.randint(len(far))]
    return np.exp2(a.ravel()).repeat(32)


def f64(x):
    return np.asarray(x).astype(np.float64)


def striped(idx):
    return np.tile(np.asarray(idx).reshape(-1, 16).T, (8, 1)).astype(np.uint16)


def unstriped(offs):
    return offs[:16].T.reshape(-1).astype(np.int64)


E2M1 = np.array([0.0, 0.5, 1.0, 1.5, 2.0, 3.0, 4.0, 6.0, -0.0, -0.5, -1.0, -1.5, -2.0, -3.0, -4.0, -6.0])


def pack_weight(w, fmt):
    k, n = w.shape
    w = f64(np.asarray(w, np.float32).astype(ml_dtypes.bfloat16)).reshape(k // 32, 32, n)
    amax = np.abs(w).max(1)
    if fmt == "e4m3":
        byte = np.frexp(amax)[1] - 1 + 127 - 7
    else:
        mant, ex = np.frexp(amax / 6.0)
        byte = np.where(mant > 0.5, ex, ex - 1) + 127
    byte = np.clip(np.where(amax > 0, byte, 1), 1, 254)
    scaled = (w * np.exp2(127.0 - byte)[:, None, :]).reshape(k, n).astype(np.float32)
    by_word = np.ascontiguousarray(scaled.reshape(k // 512, 128, 4, n).transpose(0, 1, 3, 2))
    if fmt == "e4m3":
        words = by_word.astype(ml_dtypes.float8_e4m3fn).view(np.uint8)
    else:
        c = by_word.astype(ml_dtypes.float4_e2m1fn).view(np.uint8) & 0xF
        words = (c[..., 0::2] | (c[..., 1::2] << 4)).reshape(k // 512, 128, 2 * n)
    return np.ascontiguousarray(words), np.ascontiguousarray(byte.astype(np.uint8).reshape(k // 512, 16, n))


def unpack_weight(words, scales, fmt):
    g, _, n = scales.shape
    words = np.ascontiguousarray(words).reshape(g, 128, n, -1)
    if fmt == "e4m3":
        vals = words.view(ml_dtypes.float8_e4m3fn).astype(np.float64)
    else:
        nib = np.empty((g, 128, n, 4), np.uint8)
        nib[..., 0::2] = words & 0xF
        nib[..., 1::2] = words >> 4
        vals = E2M1[nib]
    vals = vals * np.repeat(np.exp2(scales.astype(np.float64) - 127.0), 8, axis=1)[..., None]
    return vals.transpose(0, 1, 3, 2).reshape(g * 512, n)


K, R, F, T, J, G = 512, 128, 512, 2048, 512, 32


def setup_inputs():
    n = np.random.standard_normal
    idx = np.random.permutation(T)[:J]
    fk = mx_kscale(K)
    ff = mx_kscale(F)
    tabp = pack_weight(n((K, T)) / fk[:, None], "e4m3")
    return {
        "tab_words": tabp[0],
        "tab_scales": tabp[1],
        "w1": (n((K, R)) * 1 / np.sqrt(K) * fk[:, None]).astype(np.float32),
        "sharp": (np.random.uniform(0.3, 1.5, (R, 1))).astype(np.float32),
        "wo": (n((F, R)) * 1 / np.sqrt(F) * ff[:, None]).astype(np.float32),
        "dy": (n((F, J)) / ff[:, None]).astype(np.float32),
        "og": (np.random.uniform(0.3, 1.0, (R, 1))).astype(np.float32),
        "base": (0.3 * n((R, J))).astype(np.float32),
        "offs": striped(idx),
    }


def reference(tab_words, tab_scales, w1, sharp, wo, dy, og, base, offs):
    idx = unstriped(offs)
    tabu = unpack_weight(tab_words, tab_scales, "e4m3")
    w1q = mxq(f64(w1), 0, "e4m3")
    tabidxg = tabu[:, idx]
    a = w1q.T @ tabidxg
    m1 = a.reshape(R, G, J // G).mean(axis=2)
    mr = np.repeat(m1, J // G, axis=1)
    ce = a - mr
    woq = mxq(f64(wo), 0, "e4m3")
    dyq = mxq(f64(dy), 0, "e4m3")
    c0 = woq.T @ dyq
    dce = c0 * a / np.square(np.square(ce) * f64(sharp) + 1.0) * (-1.0) * f64(sharp) * ce * 2.0
    dmr = dce * (-1.0)
    dm1 = dmr.reshape(R, G, J // G).sum(axis=2)
    e1 = dm1 / 16.0
    r1 = np.repeat(e1, J // G, axis=1)
    da = c0 / (np.square(ce) * f64(sharp) + 1.0) + dce + r1
    hda = da * 2.0
    he1 = hda.reshape(R, G, J // G).sum(axis=2)
    hdm1 = he1 / 16.0
    r51 = np.repeat(hdm1, J // G, axis=1)
    hdce = hda - r51
    hce = hda * c0 / np.square(np.square(ce) * f64(sharp) + 1.0) * (-1.0) * f64(sharp) * ce * 2.0 + hdce * 2.0 * ce * f64(sharp) * (-1.0) * c0 * a / np.square(np.square(np.square(ce) * f64(sharp) + 1.0)) * (-1.0) * (np.square(ce) * f64(sharp) + 1.0) * 2.0 * f64(sharp) * ce * 2.0 + hdce * 2.0 * c0 * a / np.square(np.square(ce) * f64(sharp) + 1.0) * (-1.0) * f64(sharp)
    hmr = hce * (-1.0)
    hm1 = hmr.reshape(R, G, J // G).sum(axis=2)
    e52 = hm1 / 16.0
    r52 = np.repeat(e52, J // G, axis=1)
    ha = hdce * 2.0 * ce * f64(sharp) * (-1.0) / np.square(np.square(ce) * f64(sharp) + 1.0) * c0 + hce + r52
    y = ha * f64(og) + f64(base)
    return y

@@ -1,0 +1,213 @@
+from contextlib import ExitStack
+
+import concourse.mybir as mybir
+
+F32 = mybir.dt.float32
+BF16 = mybir.dt.bfloat16
+I32 = mybir.dt.int32
+U32 = mybir.dt.uint32
+U16 = mybir.dt.uint16
+U8 = mybir.dt.uint8
+FP8X4 = mybir.dt.float8_e4m3fn_x4
+ALU = mybir.AluOpType
+ACT = mybir.ActivationFunctionType
+AX = mybir.AxisListType
+
+P = 128
+PACK = 4
+K, R, T, J = 512, 128, 2048, 512
+GROUP = 16
+HALVES = 2
+W = J // HALVES
+GH = W // GROUP
+FLOPS = 2 * 2 * K * R * J
+
+S_HD = (False, False)
+S_Y = (True, True)
+S_FIN = (True, True)
+V_DY = (True, False)
+
+
+def interleave_views(grouped, raw):
+    return (grouped.rearrange("p (c i) t -> p c t i", i=4), raw.rearrange("p t (c i) -> p c t i", i=4))
+
+
+def grouped_view(ap):
+    return ap.rearrange("p (g i) -> p g i", i=GROUP)
+
+
+def spread(col):
+    return col.unsqueeze(2).to_broadcast([P, GH, GROUP])
+
+
+def tile_attend_gpcontrastpool_kernel(tc, tab_words, tab_scales, w1, sharp, wo, dy, og, base, offs, out):
+    nc = tc.nc
+    with ExitStack() as ctx:
+        keep = ctx.enter_context(tc.tile_pool(name="keep", bufs=1))
+        psum = ctx.enter_context(tc.psum_pool(name="psum", bufs=1))
+
+        offsets = keep.tile([P, J // 16], U16, name="offsets")
+        nc.sync.dma_start(offsets[:], offs)
+
+        scale_win = keep.tile([P, T], U8, name="scale_win", align_bytes=64)
+        nc.vector.memset(scale_win[:, : T // 2].bitcast(I32), 0)
+        nc.gpsimd.memset(scale_win[:, T // 2 :].bitcast(I32), 0)
+        warm = keep.tile([P, 1], F32, name="warm")
+        nc.vector.memset(warm[:], 1.0)
+
+        w1_raw = keep.tile([P, PACK, R], F32, name="w1_raw")
+        nc.sync.dma_start(w1_raw[:], w1.rearrange("(p t) r -> p t r", t=PACK))
+        sharp_sb = keep.tile([P, 1], F32, name="sharp_sb")
+        nc.sync.dma_start(sharp_sb[:], sharp)
+        for q in range(4):
+            nc.sync.dma_start(scale_win[32 * q : 32 * q + 4, :].bitcast(I32), tab_scales[0, 4 * q : 4 * q + 4, :].bitcast(I32))
+        word_win = keep.tile([P, T], U32, name="word_win", align_bytes=64)
+        nc.sync.dma_start(word_win[:].bitcast(I32), tab_words[0].rearrange("p n t -> p (n t)").bitcast(I32))
+        wo_raw = keep.tile([P, PACK, R], F32, name="wo_raw")
+        nc.sync.dma_start(wo_raw[:], wo.rearrange("(p t) r -> p t r", t=PACK))
+        warm_out = keep.tile([P, 1], F32, name="warm_out")
+        nc.scalar.activation(warm_out[:], warm[:], ACT.Abs_reciprocal_sqrt)
+
+        def quantise(name, grouped, width):
+            codes = keep.tile([P, width], U32, name=name + "_codes", align_bytes=64)
+            scales = keep.tile([P, width], U8, name=name + "_scales", align_bytes=64)
+            nc.vector.quantize_mx(out=codes[:].bitcast(FP8X4), scales=scales[:], in_=grouped[:].rearrange("p w t -> p (w t)"))
+            return codes, scales
+
+        def interleave(name, raw, width, on_vector):
+            grouped = keep.tile([P, width, PACK], BF16, name=name + "_bf", align_bytes=64)
+            dst, src = interleave_views(grouped[:], raw)
+            if on_vector:
+                nc.vector.tensor_copy(dst, src)
+            else:
+                nc.scalar.copy(dst, src)
+            return grouped
+
+        w1_bf = interleave("w1", w1_raw[:], R, False)
+        tab_s = keep.tile([P, J], U8, name="tab_s", align_bytes=64)
+        nc.vector.tensor_copy(tab_s[:], scale_win[:].indirect(offsets[:]))
+        w1_codes, w1_scales = quantise("w1", w1_bf, R)
+
+        dy_raw = keep.tile([P, HALVES, PACK, W], F32, name="dy_raw")
+        dy_rows = dy.rearrange("(p t) j -> p t j", t=PACK)
+        for h in range(HALVES):
+            nc.sync.dma_start(dy_raw[:, h], dy_rows[:, :, h * W : (h + 1) * W])
+
+        og_sb = keep.tile([P, 1], F32, name="og_sb")
+        nc.sync.dma_start(og_sb[:], og)
+        tab_w = keep.tile([P, J], U32, name="tab_w", align_bytes=64)
+        a_ps = []
+        for h in range(HALVES):
+            cols = slice(h * W, (h + 1) * W)
+            nc.vector.tensor_copy(tab_w[:, cols], word_win[:].indirect(offsets[:, h * GH : (h + 1) * GH]))
+            bank = psum.tile([P, W], F32, name="a_ps%d" % h)
+            nc.tensor.matmul_mx(out=bank[:], lhsT=w1_codes[:].bitcast(FP8X4), lhsT_scale=w1_scales[:],
+                                rhs=tab_w[:, cols].bitcast(FP8X4), rhs_scale=tab_s[:, cols], start=True, stop=True)
+            a_ps.append(bank)
+
+        wo_bf = interleave("wo", wo_raw[:], R, False)
+        base_sb = keep.tile([P, J], F32, name="base_sb")
+        nc.sync.dma_start(base_sb[:], base)
+
+        def new(name):
+            return [keep.tile([P, W], F32, name="%s%d" % (name, h)) for h in range(HALVES)]
+
+        def stage(fn):
+            for h in range(HALVES):
+                fn(h)
+
+        e, e2, v, u, hq = new("e"), new("e2"), new("v"), new("u"), new("hq")
+        sum_a = [keep.tile([P, GH], F32, name="sum_a%d" % h) for h in range(HALVES)]
+        for h in range(HALVES):
+            nc.vector.tensor_reduce(sum_a[h][:], grouped_view(a_ps[h][:]), AX.X, ALU.add)
+            if h == 0:
+                wo_codes, wo_scales = quantise("wo", wo_bf, R)
+            nc.vector.scalar_tensor_tensor(grouped_view(e[h][:]), spread(sum_a[h][:]), -1.0 / GROUP, grouped_view(a_ps[h][:]), ALU.mult, ALU.add)
+        for h in range(HALVES):
+            nc.scalar.activation(e2[h][:], e[h][:], ACT.Square)
+            nc.scalar.activation(v[h][:], e2[h][:], ACT.Square, bias=1.0, scale=sharp_sb[:])
+            nc.scalar.activation(u[h][:], v[h][:], ACT.Abs_reciprocal_sqrt)
+            nc.scalar.activation(hq[h][:], u[h][:], ACT.Square, bias=-0.75, scale=2.0)
+
+        c_ps = [None] * HALVES
+
+        def make_c(h):
+            dy_bf = interleave("dy%d" % h, dy_raw[:, h], W, V_DY[h])
+            codes, scales = quantise("dy%d" % h, dy_bf, W)
+            c_ps[h] = psum.tile([P, W], F32, name="c_ps%d" % h)
+            nc.tensor.matmul_mx(out=c_ps[h][:], lhsT=wo_codes[:].bitcast(FP8X4), lhsT_scale=wo_scales[:],
+                                rhs=codes[:].bitcast(FP8X4), rhs_scale=scales[:], start=True, stop=True)
+
+        make_c(0)
+        eu, aeu, aq, pq = new("eu"), new("aeu"), new("aq"), new("pq")
+        for h in range(HALVES):
+            nc.vector.scalar_tensor_tensor(eu[h][:], e[h][:], sharp_sb[:], u[h][:], ALU.mult, ALU.mult)
+            nc.vector.scalar_tensor_tensor(aq[h][:], hq[h][:], -0.5625, a_ps[h][:], ALU.add, ALU.mult)
+            nc.vector.scalar_tensor_tensor(aeu[h][:], eu[h][:], -2.0, a_ps[h][:], ALU.mult, ALU.mult)
+            nc.vector.scalar_tensor_tensor(pq[h][:], aq[h][:], sharp_sb[:], eu[h][:], ALU.mult, ALU.add)
+        make_c(1)
+
+        cut = [keep.tile([P, 2, W], F32, name="cut%d" % h) for h in range(HALVES)]
+        neg = [keep.tile([P, 2, GH], F32, name="neg%d" % h) for h in range(HALVES)]
+        pp, pqc, hd, x, yn, hh, z, o1, o2, y = [new(n) for n in ("pp", "pqc", "hd", "x", "yn", "hh", "z", "o1", "o2", "y")]
+        sum_h = [keep.tile([P, GH], F32, name="sum_h%d" % h) for h in range(HALVES)]
+
+        def per_group(dst, src, scale, bias):
+            for g in range(GH):
+                cols = slice(g * GROUP, (g + 1) * GROUP)
+                nc.scalar.activation(dst[:, cols], src[:, cols], ACT.Identity, bias=bias(g), scale=scale(g))
+
+        def op_cu(h):
+            nc.vector.scalar_tensor_tensor(cut[h][:, 0, :], c_ps[h][:], 0.125, u[h][:], ALU.mult, ALU.mult)
+
+        def op_t(h):
+            nc.vector.scalar_tensor_tensor(cut[h][:, 1, :], aeu[h][:], 1.0, cut[h][:, 0, :], ALU.add, ALU.mult)
+
+        def op_p(h):
+            nc.vector.scalar_tensor_tensor(pp[h][:], eu[h][:], og_sb[:], cut[h][:, 0, :], ALU.mult, ALU.mult)
+
+        def op_red(h):
+            nc.vector.tensor_reduce(neg[h][:], cut[h][:].rearrange("p a (g i) -> p a g i", i=GROUP), AX.X, ALU.add, negate=True)
+
+        def op_pq(h):
+            nc.vector.scalar_tensor_tensor(pqc[h][:], pq[h][:], og_sb[:], cut[h][:, 0, :], ALU.mult, ALU.mult)
+
+        def op_hd(h):
+            if S_HD[h]:
+                per_group(hd[h], cut[h][:, 1, :], lambda g: 16.0, lambda g: neg[h][:, 1, g : g + 1])
+            else:
+                nc.vector.scalar_tensor_tensor(grouped_view(hd[h][:]), grouped_view(cut[h][:, 1, :]), 16.0, spread(neg[h][:, 1, :]), ALU.mult, ALU.add)
+
+        def op_y(h):
+            if S_Y[h]:
+                per_group(yn[h], pp[h], lambda g: neg[h][:, 0, g : g + 1], lambda g: 0.0)
+            else:
+                nc.vector.tensor_tensor(grouped_view(yn[h][:]), grouped_view(pp[h][:]), spread(neg[h][:, 0, :]), ALU.mult)
+
+        def op_x(h):
+            nc.vector.tensor_tensor(x[h][:], hd[h][:], pqc[h][:], ALU.mult)
+
+        def op_z(h):
+            nc.vector.tensor_tensor(z[h][:], hd[h][:], pp[h][:], ALU.mult)
+
+        def op_h(h):
+            nc.vector.tensor_tensor(hh[h][:], x[h][:], yn[h][:], ALU.subtract)
+
+        def op_o1(h):
+            nc.vector.scalar_tensor_tensor(o1[h][:], z[h][:], -16.0, base_sb[:, h * W : (h + 1) * W], ALU.mult, ALU.add)
+
+        def op_redh(h):
+            nc.vector.tensor_reduce(sum_h[h][:], grouped_view(hh[h][:]), AX.X, ALU.add)
+
+        def op_hc(h):
+            if S_FIN[h]:
+                per_group(o2[h], hh[h], lambda g: -16.0, lambda g: sum_h[h][:, g : g + 1])
+            else:
+                nc.vector.scalar_tensor_tensor(grouped_view(o2[h][:]), grouped_view(hh[h][:]), -16.0, spread(sum_h[h][:]), ALU.mult, ALU.add)
+
+        def op_fin(h):
+            nc.vector.tensor_tensor(y[h][:], o1[h][:], o2[h][:], ALU.add)
+            nc.sync.dma_start(out[:, h * W : (h + 1) * W], y[h][:])
+
+        for fn in (op_cu, op_t, op_p, op_red, op_y, op_hd, op_pq, op_x, op_h, op_redh, op_hc, op_z, op_o1, op_fin):
+            stage(fn)

@@ -24,7 +24,7 @@ FLOPS = 2 * 2 * K * R * J
 
 S_HD = (False, False)
 S_Y = (True, True)
-S_FIN = (True, True)
+S_FIN = (True, False)
 V_DY = (True, False)
 
 
@@ -50,21 +50,20 @@ def tile_attend_gpcontrastpool_kernel(tc, tab_words, tab_scales, w1, sharp, wo, 
         nc.sync.dma_start(offsets[:], offs)
 
         scale_win = keep.tile([P, T], U8, name="scale_win", align_bytes=64)
-        nc.vector.memset(scale_win[:, : T // 2].bitcast(I32), 0)
-        nc.gpsimd.memset(scale_win[:, T // 2 :].bitcast(I32), 0)
+        nc.vector.memset(scale_win[:].bitcast(I32), 0)
         warm = keep.tile([P, 1], F32, name="warm")
         nc.vector.memset(warm[:], 1.0)
 
         w1_raw = keep.tile([P, PACK, R], F32, name="w1_raw")
         nc.sync.dma_start(w1_raw[:], w1.rearrange("(p t) r -> p t r", t=PACK))
-        sharp_sb = keep.tile([P, 1], F32, name="sharp_sb")
-        nc.sync.dma_start(sharp_sb[:], sharp)
         for q in range(4):
             nc.sync.dma_start(scale_win[32 * q : 32 * q + 4, :].bitcast(I32), tab_scales[0, 4 * q : 4 * q + 4, :].bitcast(I32))
         word_win = keep.tile([P, T], U32, name="word_win", align_bytes=64)
         nc.sync.dma_start(word_win[:].bitcast(I32), tab_words[0].rearrange("p n t -> p (n t)").bitcast(I32))
         wo_raw = keep.tile([P, PACK, R], F32, name="wo_raw")
         nc.sync.dma_start(wo_raw[:], wo.rearrange("(p t) r -> p t r", t=PACK))
+        sharp_sb = keep.tile([P, 1], F32, name="sharp_sb")
+        nc.sync.dma_start(sharp_sb[:], sharp)
         warm_out = keep.tile([P, 1], F32, name="warm_out")
         nc.scalar.activation(warm_out[:], warm[:], ACT.Abs_reciprocal_sqrt)
 
@@ -74,8 +73,8 @@ def tile_attend_gpcontrastpool_kernel(tc, tab_words, tab_scales, w1, sharp, wo, 
             nc.vector.quantize_mx(out=codes[:].bitcast(FP8X4), scales=scales[:], in_=grouped[:].rearrange("p w t -> p (w t)"))
             return codes, scales
 
-        def interleave(name, raw, width, on_vector):
-            grouped = keep.tile([P, width, PACK], BF16, name=name + "_bf", align_bytes=64)
+        def interleave(name, raw, width, on_vector, tag=None):
+            grouped = keep.tile([P, width, PACK], BF16, name=name + "_bf", tag=tag or name + "_bf", align_bytes=64)
             dst, src = interleave_views(grouped[:], raw)
             if on_vector:
                 nc.vector.tensor_copy(dst, src)
@@ -116,7 +115,8 @@ def tile_attend_gpcontrastpool_kernel(tc, tab_words, tab_scales, w1, sharp, wo, 
             for h in range(HALVES):
                 fn(h)
 
-        e, e2, v, u, hq = new("e"), new("e2"), new("v"), new("u"), new("hq")
+        e, e2, u, hq = new("e"), new("e2"), new("u"), new("hq")
+        v = [keep.tile([P, W], F32, name="v%d" % h, tag="v%d" % h, align_bytes=64) for h in range(HALVES)]
         sum_a = [keep.tile([P, GH], F32, name="sum_a%d" % h) for h in range(HALVES)]
         for h in range(HALVES):
             nc.vector.tensor_reduce(sum_a[h][:], grouped_view(a_ps[h][:]), AX.X, ALU.add)
@@ -132,7 +132,7 @@ def tile_attend_gpcontrastpool_kernel(tc, tab_words, tab_scales, w1, sharp, wo, 
         c_ps = [None] * HALVES
 
         def make_c(h):
-            dy_bf = interleave("dy%d" % h, dy_raw[:, h], W, V_DY[h])
+            dy_bf = interleave("dy%d" % h, dy_raw[:, h], W, V_DY[h], None if V_DY[h] else "v1")
             codes, scales = quantise("dy%d" % h, dy_bf, W)
             c_ps[h] = psum.tile([P, W], F32, name="c_ps%d" % h)
             nc.tensor.matmul_mx(out=c_ps[h][:], lhsT=wo_codes[:].bitcast(FP8X4), lhsT_scale=wo_scales[:],

@@ -22,10 +22,10 @@ W = J // HALVES
 GH = W // GROUP
 FLOPS = 2 * 2 * K * R * J
 
-S_HD = (False, False)
+S_HD = (True, True)
 S_Y = (True, True)
 S_FIN = (True, False)
-V_DY = (True, False)
+V_DY = (False, True)
 
 
 def interleave_views(grouped, raw):
@@ -56,14 +56,13 @@ def tile_attend_gpcontrastpool_kernel(tc, tab_words, tab_scales, w1, sharp, wo, 
 
         w1_raw = keep.tile([P, PACK, R], F32, name="w1_raw")
         nc.sync.dma_start(w1_raw[:], w1.rearrange("(p t) r -> p t r", t=PACK))
+        wo_raw = keep.tile([P, PACK, R], F32, name="wo_raw")
+        nc.sync.dma_start(wo_raw[:], wo.rearrange("(p t) r -> p t r", t=PACK))
         for q in range(4):
             nc.sync.dma_start(scale_win[32 * q : 32 * q + 4, :].bitcast(I32), tab_scales[0, 4 * q : 4 * q + 4, :].bitcast(I32))
         word_win = keep.tile([P, T], U32, name="word_win", align_bytes=64)
         nc.sync.dma_start(word_win[:].bitcast(I32), tab_words[0].rearrange("p n t -> p (n t)").bitcast(I32))
-        wo_raw = keep.tile([P, PACK, R], F32, name="wo_raw")
-        nc.sync.dma_start(wo_raw[:], wo.rearrange("(p t) r -> p t r", t=PACK))
         sharp_sb = keep.tile([P, 1], F32, name="sharp_sb")
-        nc.sync.dma_start(sharp_sb[:], sharp)
         warm_out = keep.tile([P, 1], F32, name="warm_out")
         nc.scalar.activation(warm_out[:], warm[:], ACT.Abs_reciprocal_sqrt)
 
@@ -86,11 +85,15 @@ def tile_attend_gpcontrastpool_kernel(tc, tab_words, tab_scales, w1, sharp, wo, 
         tab_s = keep.tile([P, J], U8, name="tab_s", align_bytes=64)
         nc.vector.tensor_copy(tab_s[:], scale_win[:].indirect(offsets[:]))
         w1_codes, w1_scales = quantise("w1", w1_bf, R)
+        wo_bf = interleave("wo", wo_raw[:], R, False)
+        wo_codes, wo_scales = quantise("wo", wo_bf, R)
 
         dy_raw = keep.tile([P, HALVES, PACK, W], F32, name="dy_raw")
         dy_rows = dy.rearrange("(p t) j -> p t j", t=PACK)
         for h in range(HALVES):
             nc.sync.dma_start(dy_raw[:, h], dy_rows[:, :, h * W : (h + 1) * W])
+            if h == 0:
+                nc.sync.dma_start(sharp_sb[:], sharp)
 
         og_sb = keep.tile([P, 1], F32, name="og_sb")
         nc.sync.dma_start(og_sb[:], og)
@@ -104,7 +107,6 @@ def tile_attend_gpcontrastpool_kernel(tc, tab_words, tab_scales, w1, sharp, wo, 
                                 rhs=tab_w[:, cols].bitcast(FP8X4), rhs_scale=tab_s[:, cols], start=True, stop=True)
             a_ps.append(bank)
 
-        wo_bf = interleave("wo", wo_raw[:], R, False)
         base_sb = keep.tile([P, J], F32, name="base_sb")
         nc.sync.dma_start(base_sb[:], base)
 
@@ -120,9 +122,8 @@ def tile_attend_gpcontrastpool_kernel(tc, tab_words, tab_scales, w1, sharp, wo, 
         sum_a = [keep.tile([P, GH], F32, name="sum_a%d" % h) for h in range(HALVES)]
         for h in range(HALVES):
             nc.vector.tensor_reduce(sum_a[h][:], grouped_view(a_ps[h][:]), AX.X, ALU.add)
-            if h == 0:
-                wo_codes, wo_scales = quantise("wo", wo_bf, R)
             nc.vector.scalar_tensor_tensor(grouped_view(e[h][:]), spread(sum_a[h][:]), -1.0 / GROUP, grouped_view(a_ps[h][:]), ALU.mult, ALU.add)
+        dy_bf = [interleave("dy%d" % h, dy_raw[:, h], W, V_DY[h]) for h in range(HALVES)]
         for h in range(HALVES):
             nc.scalar.activation(e2[h][:], e[h][:], ACT.Square)
             nc.scalar.activation(v[h][:], e2[h][:], ACT.Square, bias=1.0, scale=sharp_sb[:])
@@ -132,20 +133,19 @@ def tile_attend_gpcontrastpool_kernel(tc, tab_words, tab_scales, w1, sharp, wo, 
         c_ps = [None] * HALVES
 
         def make_c(h):
-            dy_bf = interleave("dy%d" % h, dy_raw[:, h], W, V_DY[h], None if V_DY[h] else "v1")
-            codes, scales = quantise("dy%d" % h, dy_bf, W)
+            codes, scales = quantise("dy%d" % h, dy_bf[h], W)
             c_ps[h] = psum.tile([P, W], F32, name="c_ps%d" % h)
             nc.tensor.matmul_mx(out=c_ps[h][:], lhsT=wo_codes[:].bitcast(FP8X4), lhsT_scale=wo_scales[:],
                                 rhs=codes[:].bitcast(FP8X4), rhs_scale=scales[:], start=True, stop=True)
 
         make_c(0)
+        make_c(1)
         eu, aeu, aq, pq = new("eu"), new("aeu"), new("aq"), new("pq")
         for h in range(HALVES):
             nc.vector.scalar_tensor_tensor(eu[h][:], e[h][:], sharp_sb[:], u[h][:], ALU.mult, ALU.mult)
             nc.vector.scalar_tensor_tensor(aq[h][:], hq[h][:], -0.5625, a_ps[h][:], ALU.add, ALU.mult)
             nc.vector.scalar_tensor_tensor(aeu[h][:], eu[h][:], -2.0, a_ps[h][:], ALU.mult, ALU.mult)
             nc.vector.scalar_tensor_tensor(pq[h][:], aq[h][:], sharp_sb[:], eu[h][:], ALU.mult, ALU.add)
-        make_c(1)
 
         cut = [keep.tile([P, 2, W], F32, name="cut%d" % h) for h in range(HALVES)]
         neg = [keep.tile([P, 2, GH], F32, name="neg%d" % h) for h in range(HALVES)]
@@ -209,5 +209,5 @@ def tile_attend_gpcontrastpool_kernel(tc, tab_words, tab_scales, w1, sharp, wo, 
             nc.vector.tensor_tensor(y[h][:], o1[h][:], o2[h][:], ALU.add)
             nc.sync.dma_start(out[:, h * W : (h + 1) * W], y[h][:])
 
-        for fn in (op_cu, op_t, op_p, op_red, op_y, op_hd, op_pq, op_x, op_h, op_redh, op_hc, op_z, op_o1, op_fin):
+        for fn in (op_cu, op_t, op_red, op_hd, op_p, op_y, op_pq, op_x, op_z, op_h, op_redh, op_hc, op_o1, op_fin):
             stage(fn)

@@ -11,33 +11,32 @@ U8 = mybir.dt.uint8
 FP8X4 = mybir.dt.float8_e4m3fn_x4
 ALU = mybir.AluOpType
 ACT = mybir.ActivationFunctionType
-AX = mybir.AxisListType
+AXIS = mybir.AxisListType
 
-P = 128
+PARTS = 128
 PACK = 4
 K, R, T, J = 512, 128, 2048, 512
+SCALE_ROWS = K // 32
+QUADRANT = 32
+LIST_ROWS = 16
+LINE = 4
 GROUP = 16
-HALVES = 2
-W = J // HALVES
-GH = W // GROUP
+HALVES = (0, 1)
+W = J // len(HALVES)
+GROUPS = W // GROUP
 FLOPS = 2 * 2 * K * R * J
 
-S_HD = (True, True)
-S_Y = (True, True)
-S_FIN = (True, False)
-V_DY = (False, True)
 
-
-def interleave_views(grouped, raw):
-    return (grouped.rearrange("p (c i) t -> p c t i", i=4), raw.rearrange("p t (c i) -> p c t i", i=4))
-
-
-def grouped_view(ap):
+def by_group(ap):
     return ap.rearrange("p (g i) -> p g i", i=GROUP)
 
 
-def spread(col):
-    return col.unsqueeze(2).to_broadcast([P, GH, GROUP])
+def spread(sums):
+    return sums.unsqueeze(2).to_broadcast([PARTS, GROUPS, GROUP])
+
+
+def half_cols(h):
+    return slice(h * W, (h + 1) * W)
 
 
 def tile_attend_gpcontrastpool_kernel(tc, tab_words, tab_scales, w1, sharp, wo, dy, og, base, offs, out):
@@ -46,168 +45,134 @@ def tile_attend_gpcontrastpool_kernel(tc, tab_words, tab_scales, w1, sharp, wo, 
         keep = ctx.enter_context(tc.tile_pool(name="keep", bufs=1))
         psum = ctx.enter_context(tc.psum_pool(name="psum", bufs=1))
 
-        offsets = keep.tile([P, J // 16], U16, name="offsets")
-        nc.sync.dma_start(offsets[:], offs)
-
-        scale_win = keep.tile([P, T], U8, name="scale_win", align_bytes=64)
-        nc.vector.memset(scale_win[:].bitcast(I32), 0)
-        warm = keep.tile([P, 1], F32, name="warm")
-        nc.vector.memset(warm[:], 1.0)
-
-        w1_raw = keep.tile([P, PACK, R], F32, name="w1_raw")
-        nc.sync.dma_start(w1_raw[:], w1.rearrange("(p t) r -> p t r", t=PACK))
-        wo_raw = keep.tile([P, PACK, R], F32, name="wo_raw")
-        nc.sync.dma_start(wo_raw[:], wo.rearrange("(p t) r -> p t r", t=PACK))
-        for q in range(4):
-            nc.sync.dma_start(scale_win[32 * q : 32 * q + 4, :].bitcast(I32), tab_scales[0, 4 * q : 4 * q + 4, :].bitcast(I32))
-        word_win = keep.tile([P, T], U32, name="word_win", align_bytes=64)
-        nc.sync.dma_start(word_win[:].bitcast(I32), tab_words[0].rearrange("p n t -> p (n t)").bitcast(I32))
-        sharp_sb = keep.tile([P, 1], F32, name="sharp_sb")
-        warm_out = keep.tile([P, 1], F32, name="warm_out")
-        nc.scalar.activation(warm_out[:], warm[:], ACT.Abs_reciprocal_sqrt)
-
-        def quantise(name, grouped, width):
-            codes = keep.tile([P, width], U32, name=name + "_codes", align_bytes=64)
-            scales = keep.tile([P, width], U8, name=name + "_scales", align_bytes=64)
-            nc.vector.quantize_mx(out=codes[:].bitcast(FP8X4), scales=scales[:], in_=grouped[:].rearrange("p w t -> p (w t)"))
-            return codes, scales
-
-        def interleave(name, raw, width, on_vector, tag=None):
-            grouped = keep.tile([P, width, PACK], BF16, name=name + "_bf", tag=tag or name + "_bf", align_bytes=64)
-            dst, src = interleave_views(grouped[:], raw)
-            if on_vector:
-                nc.vector.tensor_copy(dst, src)
-            else:
-                nc.scalar.copy(dst, src)
+        def interleave(name, raw, width, copy):
+            grouped = keep.tile([PARTS, width, PACK], BF16, name=name + "_bf", align_bytes=64)
+            copy(grouped[:].rearrange("p (c i) t -> p c t i", i=LINE), raw.rearrange("p t (c i) -> p c t i", i=LINE))
             return grouped
 
-        w1_bf = interleave("w1", w1_raw[:], R, False)
-        tab_s = keep.tile([P, J], U8, name="tab_s", align_bytes=64)
-        nc.vector.tensor_copy(tab_s[:], scale_win[:].indirect(offsets[:]))
-        w1_codes, w1_scales = quantise("w1", w1_bf, R)
-        wo_bf = interleave("wo", wo_raw[:], R, False)
-        wo_codes, wo_scales = quantise("wo", wo_bf, R)
+        def quantise(name, grouped, width):
+            words = keep.tile([PARTS, width], U32, name=name + "_words", align_bytes=64)
+            scales = keep.tile([PARTS, width], U8, name=name + "_scales", align_bytes=64)
+            nc.vector.quantize_mx(out=words[:].bitcast(FP8X4), scales=scales[:], in_=grouped[:].rearrange("p w t -> p (w t)"))
+            return words, scales
 
-        dy_raw = keep.tile([P, HALVES, PACK, W], F32, name="dy_raw")
-        dy_rows = dy.rearrange("(p t) j -> p t j", t=PACK)
-        for h in range(HALVES):
-            nc.sync.dma_start(dy_raw[:, h], dy_rows[:, :, h * W : (h + 1) * W])
-            if h == 0:
-                nc.sync.dma_start(sharp_sb[:], sharp)
+        def product(name, weight_words, weight_scales, words, scales):
+            bank = psum.tile([PARTS, W], F32, name=name)
+            nc.tensor.matmul_mx(out=bank[:], lhsT=weight_words[:].bitcast(FP8X4), lhsT_scale=weight_scales[:],
+                                rhs=words.bitcast(FP8X4), rhs_scale=scales, start=True, stop=True)
+            return bank
 
-        og_sb = keep.tile([P, 1], F32, name="og_sb")
-        nc.sync.dma_start(og_sb[:], og)
-        tab_w = keep.tile([P, J], U32, name="tab_w", align_bytes=64)
-        a_ps = []
-        for h in range(HALVES):
-            cols = slice(h * W, (h + 1) * W)
-            nc.vector.tensor_copy(tab_w[:, cols], word_win[:].indirect(offsets[:, h * GH : (h + 1) * GH]))
-            bank = psum.tile([P, W], F32, name="a_ps%d" % h)
-            nc.tensor.matmul_mx(out=bank[:], lhsT=w1_codes[:].bitcast(FP8X4), lhsT_scale=w1_scales[:],
-                                rhs=tab_w[:, cols].bitcast(FP8X4), rhs_scale=tab_s[:, cols], start=True, stop=True)
-            a_ps.append(bank)
-
-        base_sb = keep.tile([P, J], F32, name="base_sb")
-        nc.sync.dma_start(base_sb[:], base)
-
-        def new(name):
-            return [keep.tile([P, W], F32, name="%s%d" % (name, h)) for h in range(HALVES)]
-
-        def stage(fn):
-            for h in range(HALVES):
-                fn(h)
-
-        e, e2, u, hq = new("e"), new("e2"), new("u"), new("hq")
-        v = [keep.tile([P, W], F32, name="v%d" % h, tag="v%d" % h, align_bytes=64) for h in range(HALVES)]
-        sum_a = [keep.tile([P, GH], F32, name="sum_a%d" % h) for h in range(HALVES)]
-        for h in range(HALVES):
-            nc.vector.tensor_reduce(sum_a[h][:], grouped_view(a_ps[h][:]), AX.X, ALU.add)
-            nc.vector.scalar_tensor_tensor(grouped_view(e[h][:]), spread(sum_a[h][:]), -1.0 / GROUP, grouped_view(a_ps[h][:]), ALU.mult, ALU.add)
-        dy_bf = [interleave("dy%d" % h, dy_raw[:, h], W, V_DY[h]) for h in range(HALVES)]
-        for h in range(HALVES):
-            nc.scalar.activation(e2[h][:], e[h][:], ACT.Square)
-            nc.scalar.activation(v[h][:], e2[h][:], ACT.Square, bias=1.0, scale=sharp_sb[:])
-            nc.scalar.activation(u[h][:], v[h][:], ACT.Abs_reciprocal_sqrt)
-            nc.scalar.activation(hq[h][:], u[h][:], ACT.Square, bias=-0.75, scale=2.0)
-
-        c_ps = [None] * HALVES
-
-        def make_c(h):
-            codes, scales = quantise("dy%d" % h, dy_bf[h], W)
-            c_ps[h] = psum.tile([P, W], F32, name="c_ps%d" % h)
-            nc.tensor.matmul_mx(out=c_ps[h][:], lhsT=wo_codes[:].bitcast(FP8X4), lhsT_scale=wo_scales[:],
-                                rhs=codes[:].bitcast(FP8X4), rhs_scale=scales[:], start=True, stop=True)
-
-        make_c(0)
-        make_c(1)
-        eu, aeu, aq, pq = new("eu"), new("aeu"), new("aq"), new("pq")
-        for h in range(HALVES):
-            nc.vector.scalar_tensor_tensor(eu[h][:], e[h][:], sharp_sb[:], u[h][:], ALU.mult, ALU.mult)
-            nc.vector.scalar_tensor_tensor(aq[h][:], hq[h][:], -0.5625, a_ps[h][:], ALU.add, ALU.mult)
-            nc.vector.scalar_tensor_tensor(aeu[h][:], eu[h][:], -2.0, a_ps[h][:], ALU.mult, ALU.mult)
-            nc.vector.scalar_tensor_tensor(pq[h][:], aq[h][:], sharp_sb[:], eu[h][:], ALU.mult, ALU.add)
-
-        cut = [keep.tile([P, 2, W], F32, name="cut%d" % h) for h in range(HALVES)]
-        neg = [keep.tile([P, 2, GH], F32, name="neg%d" % h) for h in range(HALVES)]
-        pp, pqc, hd, x, yn, hh, z, o1, o2, y = [new(n) for n in ("pp", "pqc", "hd", "x", "yn", "hh", "z", "o1", "o2", "y")]
-        sum_h = [keep.tile([P, GH], F32, name="sum_h%d" % h) for h in range(HALVES)]
+        def halves(name, width=W):
+            return [keep.tile([PARTS, width], F32, name="%s%d" % (name, h)) for h in HALVES]
 
         def per_group(dst, src, scale, bias):
-            for g in range(GH):
+            for g in range(GROUPS):
                 cols = slice(g * GROUP, (g + 1) * GROUP)
                 nc.scalar.activation(dst[:, cols], src[:, cols], ACT.Identity, bias=bias(g), scale=scale(g))
 
-        def op_cu(h):
-            nc.vector.scalar_tensor_tensor(cut[h][:, 0, :], c_ps[h][:], 0.125, u[h][:], ALU.mult, ALU.mult)
+        offsets = keep.tile([PARTS, J // LIST_ROWS], U16, name="offsets")
+        nc.sync.dma_start(offsets[:], offs)
 
-        def op_t(h):
-            nc.vector.scalar_tensor_tensor(cut[h][:, 1, :], aeu[h][:], 1.0, cut[h][:, 0, :], ALU.add, ALU.mult)
+        table_scales = keep.tile([PARTS, T], U8, name="table_scales", align_bytes=64)
+        nc.vector.memset(table_scales[:].bitcast(I32), 0)
+        warm_in = keep.tile([PARTS, 1], F32, name="warm_in")
+        nc.vector.memset(warm_in[:], 1.0)
 
-        def op_p(h):
-            nc.vector.scalar_tensor_tensor(pp[h][:], eu[h][:], og_sb[:], cut[h][:, 0, :], ALU.mult, ALU.mult)
+        w1_raw = keep.tile([PARTS, PACK, R], F32, name="w1_raw")
+        nc.sync.dma_start(w1_raw[:], w1.rearrange("(p t) r -> p t r", t=PACK))
+        wo_raw = keep.tile([PARTS, PACK, R], F32, name="wo_raw")
+        nc.sync.dma_start(wo_raw[:], wo.rearrange("(p t) r -> p t r", t=PACK))
+        for i in range(PACK):
+            nc.sync.dma_start(table_scales[i:PARTS:QUADRANT, :].bitcast(I32), tab_scales[0, i:SCALE_ROWS:PACK, :].bitcast(I32))
+        table_words = keep.tile([PARTS, T], U32, name="table_words", align_bytes=64)
+        nc.sync.dma_start(table_words[:].bitcast(I32), tab_words[0].rearrange("p n t -> p (n t)").bitcast(I32))
 
-        def op_red(h):
-            nc.vector.tensor_reduce(neg[h][:], cut[h][:].rearrange("p a (g i) -> p a g i", i=GROUP), AX.X, ALU.add, negate=True)
+        warm_out = keep.tile([PARTS, 1], F32, name="warm_out")
+        nc.scalar.activation(warm_out[:], warm_in[:], ACT.Abs_reciprocal_sqrt)
 
-        def op_pq(h):
-            nc.vector.scalar_tensor_tensor(pqc[h][:], pq[h][:], og_sb[:], cut[h][:, 0, :], ALU.mult, ALU.mult)
+        w1_bf = interleave("w1", w1_raw[:], R, nc.scalar.copy)
+        picked_scales = keep.tile([PARTS, J], U8, name="picked_scales", align_bytes=64)
+        nc.vector.tensor_copy(picked_scales[:], table_scales[:].indirect(offsets[:]))
+        w1_words, w1_scales = quantise("w1", w1_bf, R)
+        wo_bf = interleave("wo", wo_raw[:], R, nc.scalar.copy)
+        wo_words, wo_scales = quantise("wo", wo_bf, R)
 
-        def op_hd(h):
-            if S_HD[h]:
-                per_group(hd[h], cut[h][:, 1, :], lambda g: 16.0, lambda g: neg[h][:, 1, g : g + 1])
-            else:
-                nc.vector.scalar_tensor_tensor(grouped_view(hd[h][:]), grouped_view(cut[h][:, 1, :]), 16.0, spread(neg[h][:, 1, :]), ALU.mult, ALU.add)
+        dy_raw = keep.tile([PARTS, len(HALVES), PACK, W], F32, name="dy_raw")
+        dy_rows = dy.rearrange("(p t) j -> p t j", t=PACK)
+        sharp_col = keep.tile([PARTS, 1], F32, name="sharp_col")
+        og_col = keep.tile([PARTS, 1], F32, name="og_col")
+        nc.sync.dma_start(dy_raw[:, 0], dy_rows[:, :, half_cols(0)])
+        nc.sync.dma_start(sharp_col[:], sharp)
+        nc.sync.dma_start(dy_raw[:, 1], dy_rows[:, :, half_cols(1)])
+        nc.sync.dma_start(og_col[:], og)
 
-        def op_y(h):
-            if S_Y[h]:
-                per_group(yn[h], pp[h], lambda g: neg[h][:, 0, g : g + 1], lambda g: 0.0)
-            else:
-                nc.vector.tensor_tensor(grouped_view(yn[h][:]), grouped_view(pp[h][:]), spread(neg[h][:, 0, :]), ALU.mult)
+        picked_words = keep.tile([PARTS, J], U32, name="picked_words", align_bytes=64)
+        list_cols = W // LIST_ROWS
+        a = []
+        for h in HALVES:
+            nc.vector.tensor_copy(picked_words[:, half_cols(h)], table_words[:].indirect(offsets[:, h * list_cols : (h + 1) * list_cols]))
+            a.append(product("a%d" % h, w1_words, w1_scales, picked_words[:, half_cols(h)], picked_scales[:, half_cols(h)]))
 
-        def op_x(h):
-            nc.vector.tensor_tensor(x[h][:], hd[h][:], pqc[h][:], ALU.mult)
+        base_rows = keep.tile([PARTS, J], F32, name="base_rows")
+        nc.sync.dma_start(base_rows[:], base)
 
-        def op_z(h):
-            nc.vector.tensor_tensor(z[h][:], hd[h][:], pp[h][:], ALU.mult)
+        e, sum_a = halves("e"), halves("sum_a", GROUPS)
+        for h in HALVES:
+            nc.vector.tensor_reduce(sum_a[h][:], by_group(a[h][:]), AXIS.X, ALU.add)
+            nc.vector.scalar_tensor_tensor(by_group(e[h][:]), spread(sum_a[h][:]), -1.0 / GROUP, by_group(a[h][:]), ALU.mult, ALU.add)
 
-        def op_h(h):
-            nc.vector.tensor_tensor(hh[h][:], x[h][:], yn[h][:], ALU.subtract)
+        dy_bf = [interleave("dy0", dy_raw[:, 0], W, nc.scalar.copy), interleave("dy1", dy_raw[:, 1], W, nc.vector.tensor_copy)]
 
-        def op_o1(h):
-            nc.vector.scalar_tensor_tensor(o1[h][:], z[h][:], -16.0, base_sb[:, h * W : (h + 1) * W], ALU.mult, ALU.add)
+        e_sq, d_sq, u, u_poly = halves("e_sq"), halves("d_sq"), halves("u"), halves("u_poly")
+        for h in HALVES:
+            nc.scalar.activation(e_sq[h][:], e[h][:], ACT.Square)
+            nc.scalar.activation(d_sq[h][:], e_sq[h][:], ACT.Square, bias=1.0, scale=sharp_col[:])
+            nc.scalar.activation(u[h][:], d_sq[h][:], ACT.Abs_reciprocal_sqrt)
+            nc.scalar.activation(u_poly[h][:], u[h][:], ACT.Square, bias=-0.75, scale=2.0)
 
-        def op_redh(h):
-            nc.vector.tensor_reduce(sum_h[h][:], grouped_view(hh[h][:]), AX.X, ALU.add)
+        c = []
+        for h in HALVES:
+            dy_words, dy_scales = quantise("dy%d" % h, dy_bf[h], W)
+            c.append(product("c%d" % h, wo_words, wo_scales, dy_words[:], dy_scales[:]))
 
-        def op_hc(h):
-            if S_FIN[h]:
-                per_group(o2[h], hh[h], lambda g: -16.0, lambda g: sum_h[h][:, g : g + 1])
-            else:
-                nc.vector.scalar_tensor_tensor(grouped_view(o2[h][:]), grouped_view(hh[h][:]), -16.0, spread(sum_h[h][:]), ALU.mult, ALU.add)
+        cu, seu, neg_sum_cu, saeu, p, neg_p_mean, a_poly = (halves("cu"), halves("seu"), halves("neg_sum_cu", GROUPS), halves("saeu"),
+                                                            halves("p"), halves("neg_p_mean"), halves("a_poly"))
+        for h in HALVES:
+            nc.vector.scalar_tensor_tensor(cu[h][:], c[h][:], 0.125, u[h][:], ALU.mult, ALU.mult)
+            nc.vector.scalar_tensor_tensor(seu[h][:], e[h][:], sharp_col[:], u[h][:], ALU.mult, ALU.mult)
+            nc.vector.tensor_reduce(neg_sum_cu[h][:], by_group(cu[h][:]), AXIS.X, ALU.add, negate=True)
+            nc.vector.scalar_tensor_tensor(saeu[h][:], seu[h][:], -2.0, a[h][:], ALU.mult, ALU.mult)
+            nc.vector.scalar_tensor_tensor(p[h][:], seu[h][:], og_col[:], cu[h][:], ALU.mult, ALU.mult)
+            per_group(neg_p_mean[h], p[h], lambda g: neg_sum_cu[h][:, g : g + 1], lambda g: 0.0)
+            nc.vector.scalar_tensor_tensor(a_poly[h][:], u_poly[h][:], -0.5625, a[h][:], ALU.add, ALU.mult)
 
-        def op_fin(h):
-            nc.vector.tensor_tensor(y[h][:], o1[h][:], o2[h][:], ALU.add)
-            nc.sync.dma_start(out[:, h * W : (h + 1) * W], y[h][:])
+        t, neg_sum_t, hd, pq_factor, pq = halves("t"), halves("neg_sum_t", GROUPS), halves("hd"), halves("pq_factor"), halves("pq")
+        for h in HALVES:
+            nc.vector.scalar_tensor_tensor(t[h][:], saeu[h][:], 1.0, cu[h][:], ALU.add, ALU.mult)
+        for h in HALVES:
+            nc.vector.tensor_reduce(neg_sum_t[h][:], by_group(t[h][:]), AXIS.X, ALU.add, negate=True)
+        for h in HALVES:
+            per_group(hd[h], t[h], lambda g: float(GROUP), lambda g: neg_sum_t[h][:, g : g + 1])
+        for h in HALVES:
+            nc.vector.scalar_tensor_tensor(pq_factor[h][:], a_poly[h][:], sharp_col[:], seu[h][:], ALU.mult, ALU.add)
+        for h in HALVES:
+            nc.vector.scalar_tensor_tensor(pq[h][:], pq_factor[h][:], og_col[:], cu[h][:], ALU.mult, ALU.mult)
 
-        for fn in (op_cu, op_t, op_red, op_hd, op_p, op_y, op_pq, op_x, op_z, op_h, op_redh, op_hc, op_o1, op_fin):
-            stage(fn)
+        hd_pq, hd_p, big_h, sum_h = halves("hd_pq"), halves("hd_p"), halves("big_h"), halves("sum_h", GROUPS)
+        for h in HALVES:
+            nc.vector.tensor_tensor(hd_pq[h][:], hd[h][:], pq[h][:], ALU.mult)
+        for h in HALVES:
+            nc.vector.tensor_tensor(hd_p[h][:], hd[h][:], p[h][:], ALU.mult)
+        for h in HALVES:
+            nc.vector.tensor_tensor(big_h[h][:], hd_pq[h][:], neg_p_mean[h][:], ALU.subtract)
+        for h in HALVES:
+            nc.vector.tensor_reduce(sum_h[h][:], by_group(big_h[h][:]), AXIS.X, ALU.add)
+
+        centred_h, based, result = halves("centred_h"), halves("based"), halves("result")
+        per_group(centred_h[0], big_h[0], lambda g: -float(GROUP), lambda g: sum_h[0][:, g : g + 1])
+        nc.vector.scalar_tensor_tensor(by_group(centred_h[1][:]), by_group(big_h[1][:]), -float(GROUP), spread(sum_h[1][:]), ALU.mult, ALU.add)
+        for h in HALVES:
+            nc.vector.scalar_tensor_tensor(based[h][:], hd_p[h][:], -float(GROUP), base_rows[:, half_cols(h)], ALU.mult, ALU.add)
+        for h in HALVES:
+            nc.vector.tensor_tensor(result[h][:], based[h][:], centred_h[h][:], ALU.add)
+            nc.sync.dma_start(out[:, half_cols(h)], result[h][:])

from contextlib import ExitStack

import concourse.mybir as mybir

F32 = mybir.dt.float32
BF16 = mybir.dt.bfloat16
I32 = mybir.dt.int32
U32 = mybir.dt.uint32
U16 = mybir.dt.uint16
U8 = mybir.dt.uint8
FP8X4 = mybir.dt.float8_e4m3fn_x4
ALU = mybir.AluOpType
ACT = mybir.ActivationFunctionType
AXIS = mybir.AxisListType

PARTS = 128
PACK = 4
K, R, T, J = 512, 128, 2048, 512
SCALE_ROWS = K // 32
QUADRANT = 32
LIST_ROWS = 16
LINE = 4
GROUP = 16
HALVES = (0, 1)
W = J // len(HALVES)
GROUPS = W // GROUP
FLOPS = 2 * 2 * K * R * J


def by_group(ap):
    return ap.rearrange("p (g i) -> p g i", i=GROUP)


def spread(sums):
    return sums.unsqueeze(2).to_broadcast([PARTS, GROUPS, GROUP])


def half_cols(h):
    return slice(h * W, (h + 1) * W)


def tile_attend_gpcontrastpool_kernel(tc, tab_words, tab_scales, w1, sharp, wo, dy, og, base, offs, out):
    nc = tc.nc
    with ExitStack() as ctx:
        keep = ctx.enter_context(tc.tile_pool(name="keep", bufs=1))
        psum = ctx.enter_context(tc.psum_pool(name="psum", bufs=1))

        def interleave(name, raw, width, copy):
            grouped = keep.tile([PARTS, width, PACK], BF16, name=name + "_bf", align_bytes=64)
            copy(grouped[:].rearrange("p (c i) t -> p c t i", i=LINE), raw.rearrange("p t (c i) -> p c t i", i=LINE))
            return grouped

        def quantise(name, grouped, width):
            words = keep.tile([PARTS, width], U32, name=name + "_words", align_bytes=64)
            scales = keep.tile([PARTS, width], U8, name=name + "_scales", align_bytes=64)
            nc.vector.quantize_mx(out=words[:].bitcast(FP8X4), scales=scales[:], in_=grouped[:].rearrange("p w t -> p (w t)"))
            return words, scales

        def product(name, weight_words, weight_scales, words, scales):
            bank = psum.tile([PARTS, W], F32, name=name)
            nc.tensor.matmul_mx(out=bank[:], lhsT=weight_words[:].bitcast(FP8X4), lhsT_scale=weight_scales[:],
                                rhs=words.bitcast(FP8X4), rhs_scale=scales, start=True, stop=True)
            return bank

        def halves(name, width=W):
            return [keep.tile([PARTS, width], F32, name="%s%d" % (name, h)) for h in HALVES]

        def per_group(dst, src, scale, bias):
            for g in range(GROUPS):
                cols = slice(g * GROUP, (g + 1) * GROUP)
                nc.scalar.activation(dst[:, cols], src[:, cols], ACT.Identity, bias=bias(g), scale=scale(g))

        offsets = keep.tile([PARTS, J // LIST_ROWS], U16, name="offsets")
        nc.sync.dma_start(offsets[:], offs)

        table_scales = keep.tile([PARTS, T], U8, name="table_scales", align_bytes=64)
        nc.vector.memset(table_scales[:].bitcast(I32), 0)
        warm_in = keep.tile([PARTS, 1], F32, name="warm_in")
        nc.vector.memset(warm_in[:], 1.0)

        w1_raw = keep.tile([PARTS, PACK, R], F32, name="w1_raw")
        nc.sync.dma_start(w1_raw[:], w1.rearrange("(p t) r -> p t r", t=PACK))
        wo_raw = keep.tile([PARTS, PACK, R], F32, name="wo_raw")
        nc.sync.dma_start(wo_raw[:], wo.rearrange("(p t) r -> p t r", t=PACK))
        for i in range(PACK):
            nc.sync.dma_start(table_scales[i:PARTS:QUADRANT, :].bitcast(I32), tab_scales[0, i:SCALE_ROWS:PACK, :].bitcast(I32))
        table_words = keep.tile([PARTS, T], U32, name="table_words", align_bytes=64)
        nc.sync.dma_start(table_words[:].bitcast(I32), tab_words[0].rearrange("p n t -> p (n t)").bitcast(I32))

        warm_out = keep.tile([PARTS, 1], F32, name="warm_out")
        nc.scalar.activation(warm_out[:], warm_in[:], ACT.Abs_reciprocal_sqrt)

        w1_bf = interleave("w1", w1_raw[:], R, nc.scalar.copy)
        picked_scales = keep.tile([PARTS, J], U8, name="picked_scales", align_bytes=64)
        nc.vector.tensor_copy(picked_scales[:], table_scales[:].indirect(offsets[:]))
        w1_words, w1_scales = quantise("w1", w1_bf, R)
        wo_bf = interleave("wo", wo_raw[:], R, nc.scalar.copy)
        wo_words, wo_scales = quantise("wo", wo_bf, R)

        dy_raw = keep.tile([PARTS, len(HALVES), PACK, W], F32, name="dy_raw")
        dy_rows = dy.rearrange("(p t) j -> p t j", t=PACK)
        sharp_col = keep.tile([PARTS, 1], F32, name="sharp_col")
        og_col = keep.tile([PARTS, 1], F32, name="og_col")
        nc.sync.dma_start(dy_raw[:, 0], dy_rows[:, :, half_cols(0)])
        nc.sync.dma_start(sharp_col[:], sharp)
        nc.sync.dma_start(dy_raw[:, 1], dy_rows[:, :, half_cols(1)])
        nc.sync.dma_start(og_col[:], og)

        picked_words = keep.tile([PARTS, J], U32, name="picked_words", align_bytes=64)
        list_cols = W // LIST_ROWS
        a = []
        for h in HALVES:
            nc.vector.tensor_copy(picked_words[:, half_cols(h)], table_words[:].indirect(offsets[:, h * list_cols : (h + 1) * list_cols]))
            a.append(product("a%d" % h, w1_words, w1_scales, picked_words[:, half_cols(h)], picked_scales[:, half_cols(h)]))

        base_rows = keep.tile([PARTS, J], F32, name="base_rows")
        nc.sync.dma_start(base_rows[:], base)

        e, sum_a = halves("e"), halves("sum_a", GROUPS)
        for h in HALVES:
            nc.vector.tensor_reduce(sum_a[h][:], by_group(a[h][:]), AXIS.X, ALU.add)
            nc.vector.scalar_tensor_tensor(by_group(e[h][:]), spread(sum_a[h][:]), -1.0 / GROUP, by_group(a[h][:]), ALU.mult, ALU.add)

        dy_bf = [interleave("dy0", dy_raw[:, 0], W, nc.scalar.copy), interleave("dy1", dy_raw[:, 1], W, nc.vector.tensor_copy)]

        e_sq, d_sq, u, u_poly = halves("e_sq"), halves("d_sq"), halves("u"), halves("u_poly")
        for h in HALVES:
            nc.scalar.activation(e_sq[h][:], e[h][:], ACT.Square)
            nc.scalar.activation(d_sq[h][:], e_sq[h][:], ACT.Square, bias=1.0, scale=sharp_col[:])
            nc.scalar.activation(u[h][:], d_sq[h][:], ACT.Abs_reciprocal_sqrt)
            nc.scalar.activation(u_poly[h][:], u[h][:], ACT.Square, bias=-0.75, scale=2.0)

        c = []
        for h in HALVES:
            dy_words, dy_scales = quantise("dy%d" % h, dy_bf[h], W)
            c.append(product("c%d" % h, wo_words, wo_scales, dy_words[:], dy_scales[:]))

        cu, seu, neg_sum_cu, saeu, p, neg_p_mean, a_poly = (halves("cu"), halves("seu"), halves("neg_sum_cu", GROUPS), halves("saeu"),
                                                            halves("p"), halves("neg_p_mean"), halves("a_poly"))
        for h in HALVES:
            nc.vector.scalar_tensor_tensor(cu[h][:], c[h][:], 0.125, u[h][:], ALU.mult, ALU.mult)
            nc.vector.scalar_tensor_tensor(seu[h][:], e[h][:], sharp_col[:], u[h][:], ALU.mult, ALU.mult)
            nc.vector.tensor_reduce(neg_sum_cu[h][:], by_group(cu[h][:]), AXIS.X, ALU.add, negate=True)
            nc.vector.scalar_tensor_tensor(saeu[h][:], seu[h][:], -2.0, a[h][:], ALU.mult, ALU.mult)
            nc.vector.scalar_tensor_tensor(p[h][:], seu[h][:], og_col[:], cu[h][:], ALU.mult, ALU.mult)
            per_group(neg_p_mean[h], p[h], lambda g: neg_sum_cu[h][:, g : g + 1], lambda g: 0.0)
            nc.vector.scalar_tensor_tensor(a_poly[h][:], u_poly[h][:], -0.5625, a[h][:], ALU.add, ALU.mult)

        t, neg_sum_t, hd, pq_factor, pq = halves("t"), halves("neg_sum_t", GROUPS), halves("hd"), halves("pq_factor"), halves("pq")
        for h in HALVES:
            nc.vector.scalar_tensor_tensor(t[h][:], saeu[h][:], 1.0, cu[h][:], ALU.add, ALU.mult)
        for h in HALVES:
            nc.vector.tensor_reduce(neg_sum_t[h][:], by_group(t[h][:]), AXIS.X, ALU.add, negate=True)
        for h in HALVES:
            per_group(hd[h], t[h], lambda g: float(GROUP), lambda g: neg_sum_t[h][:, g : g + 1])
        for h in HALVES:
            nc.vector.scalar_tensor_tensor(pq_factor[h][:], a_poly[h][:], sharp_col[:], seu[h][:], ALU.mult, ALU.add)
        for h in HALVES:
            nc.vector.scalar_tensor_tensor(pq[h][:], pq_factor[h][:], og_col[:], cu[h][:], ALU.mult, ALU.mult)

        hd_pq, hd_p, big_h, sum_h = halves("hd_pq"), halves("hd_p"), halves("big_h"), halves("sum_h", GROUPS)
        for h in HALVES:
            nc.vector.tensor_tensor(hd_pq[h][:], hd[h][:], pq[h][:], ALU.mult)
        for h in HALVES:
            nc.vector.tensor_tensor(hd_p[h][:], hd[h][:], p[h][:], ALU.mult)
        for h in HALVES:
            nc.vector.tensor_tensor(big_h[h][:], hd_pq[h][:], neg_p_mean[h][:], ALU.subtract)
        for h in HALVES:
            nc.vector.tensor_reduce(sum_h[h][:], by_group(big_h[h][:]), AXIS.X, ALU.add)

        centred_h, based, result = halves("centred_h"), halves("based"), halves("result")
        per_group(centred_h[0], big_h[0], lambda g: -float(GROUP), lambda g: sum_h[0][:, g : g + 1])
        nc.vector.scalar_tensor_tensor(by_group(centred_h[1][:]), by_group(big_h[1][:]), -float(GROUP), spread(sum_h[1][:]), ALU.mult, ALU.add)
        for h in HALVES:
            nc.vector.scalar_tensor_tensor(based[h][:], hd_p[h][:], -float(GROUP), base_rows[:, half_cols(h)], ALU.mult, ALU.add)
        for h in HALVES:
            nc.vector.tensor_tensor(result[h][:], based[h][:], centred_h[h][:], ALU.add)
            nc.sync.dma_start(out[:, half_cols(h)], result[h][:])
